import numpy as np
import ml_dtypes


def mxq(x, axis, fmt="e4m3"):
    dtype, down = {"e4m3": (ml_dtypes.float8_e4m3fn, 7), "e5m2": (ml_dtypes.float8_e5m2, 14)}[fmt]
    v = np.moveaxis(np.asarray(x, np.float32).astype(ml_dtypes.bfloat16).astype(np.float64), axis, -1)
    blocks = v.reshape(v.shape[:-1] + (-1, 32))
    amax = np.abs(blocks).max(-1, keepdims=True)
    byte = np.maximum(np.where(amax > 0, np.frexp(amax)[1] - 1 + 127, 0) - down, 1)
    scale = np.exp2(byte - 127.0)
    codes = (blocks / scale).astype(np.float32).astype(dtype).astype(np.float64)
    return np.moveaxis((codes * scale).reshape(v.shape), -1, axis)


WIDE = False


def mx_kscale(k):
    if not WIDE:
        return np.ones(k)
    levels = np.array([10, -10, 5, -5, 0])
    if k % 512:
        return np.exp2(np.random.permutation(np.resize(levels, k // 32))).repeat(32)
    a = np.empty((k // 512, 16))
    for p in range(k // 512):
        a[p, :8] = np.random.permutation(np.resize(levels, 8))
        for g in range(8):
            far = levels[np.abs(levels - a[p, g]) >= 10]
            a[p, g + 8] = far[np.random.randint(len(far))]
    return np.exp2(a.ravel()).repeat(32)


def f64(x):
    return np.asarray(x).astype(np.float64)


def striped(idx):
    return np.tile(np.asarray(idx).reshape(-1, 16).T, (8, 1)).astype(np.uint16)


def unstriped(offs):
    return offs[:16].T.reshape(-1).astype(np.int64)


E2M1 = np.array([0.0, 0.5, 1.0, 1.5, 2.0, 3.0, 4.0, 6.0, -0.0, -0.5, -1.0, -1.5, -2.0, -3.0, -4.0, -6.0])


def pack_weight(w, fmt):
    k, n = w.shape
    w = f64(np.asarray(w, np.float32).astype(ml_dtypes.bfloat16)).reshape(k // 32, 32, n)
    amax = np.abs(w).max(1)
    if fmt == "e4m3":
        byte = np.frexp(amax)[1] - 1 + 127 - 7
    else:
        mant, ex = np.frexp(amax / 6.0)
        byte = np.where(mant > 0.5, ex, ex - 1) + 127
    byte = np.clip(np.where(amax > 0, byte, 1), 1, 254)
    scaled = (w * np.exp2(127.0 - byte)[:, None, :]).reshape(k, n).astype(np.float32)
    by_word = np.ascontiguousarray(scaled.reshape(k // 512, 128, 4, n).transpose(0, 1, 3, 2))
    if fmt == "e4m3":
        words = by_word.astype(ml_dtypes.float8_e4m3fn).view(np.uint8)
    else:
        c = by_word.astype(ml_dtypes.float4_e2m1fn).view(np.uint8) & 0xF
        words = (c[..., 0::2] | (c[..., 1::2] << 4)).reshape(k // 512, 128, 2 * n)
    return np.ascontiguousarray(words), np.ascontiguousarray(byte.astype(np.uint8).reshape(k // 512, 16, n))


def unpack_weight(words, scales, fmt):
    g, _, n = scales.shape
    words = np.ascontiguousarray(words).reshape(g, 128, n, -1)
    if fmt == "e4m3":
        vals = words.view(ml_dtypes.float8_e4m3fn).astype(np.float64)
    else:
        nib = np.empty((g, 128, n, 4), np.uint8)
        nib[..., 0::2] = words & 0xF
        nib[..., 1::2] = words >> 4
        vals = E2M1[nib]
    vals = vals * np.repeat(np.exp2(scales.astype(np.float64) - 127.0), 8, axis=1)[..., None]
    return vals.transpose(0, 1, 3, 2).reshape(g * 512, n)


D, K, E, T, I, Q = 512, 1024, 512, 1024, 256, 128


def setup_inputs():
    n = np.random.standard_normal
    idx = np.random.permutation(T)[:I]
    fd = mx_kscale(D)
    fk = mx_kscale(K)
    fe = mx_kscale(E)
    fkeysp = pack_weight(n((K, T)) / fk[:, None], "e4m3")
    return {
        "query": (n((D, Q)) * 0.4 / np.sqrt(D) * fd[:, None]).astype(np.float32),
        "fquery": (n((K, Q)) * 1.2 / np.sqrt(K) * fk[:, None]).astype(np.float32),
        "ckeys": (n((D, T)) / fd[:, None]).astype(np.float32),
        "fkeys_words": fkeysp[0],
        "fkeys_scales": fkeysp[1],
        "share": (np.random.uniform(0.3, 0.9, (Q, 1))).astype(np.float32),
        "gout": (n((E, Q)) * 1 / np.sqrt(E) * fe[:, None]).astype(np.float32),
        "vals": (n((E, T)) / fe[:, None]).astype(np.float32),
        "fac": (np.random.uniform(0.5, 2.0, (1, T))).astype(np.float32),
        "old": (0.5 * n((Q, T))).astype(np.float32),
        "offs": striped(idx),
    }


def reference(query, fquery, ckeys, fkeys_words, fkeys_scales, share, gout, vals, fac, old, offs):
    idx = unstriped(offs)
    fkeysu = unpack_weight(fkeys_words, fkeys_scales, "e4m3")
    queryq = mxq(f64(query), 0, "e4m3")
    ckeysq = mxq(f64(ckeys), 0, "e4m3")
    a = queryq.T @ ckeysq
    fqueryq = mxq(f64(fquery), 0, "e4m3")
    fkeysidxg = fkeysu[:, idx]
    b = fqueryq.T @ fkeysidxg
    dl = (b - a[:, idx]) * f64(share)
    df1 = np.zeros((Q, T))
    df1[:, idx] = dl
    s = a + df1
    p = np.exp(s - np.max(s, axis=1, keepdims=True))
    z = np.sum(p, axis=1, keepdims=True)
    goutq = mxq(f64(gout), 0, "e4m3")
    valsq = mxq(f64(vals), 0, "e4m3")
    c0 = goutq.T @ valsq
    dz = np.sum(c0 * p * f64(fac) / np.square(z) * (-1.0), axis=1, keepdims=True)
    dp = c0 / z * f64(fac) + dz
    ds = dp * p
    ddl = ds[:, idx]
    e1 = ddl * f64(share) * (-1.0)
    s1 = np.zeros((Q, T))
    s1[:, idx] = e1
    da = ds + s1
    y = da * 1024.0 + f64(old)
    return y

@@ -1,0 +1,237 @@
+from contextlib import ExitStack
+
+import concourse.mybir as mybir
+from concourse.masks import make_identity
+
+D, K, E, T, I, Q = 512, 1024, 512, 1024, 256, 128
+FLOPS = 2 * Q * (D * T + K * I + E * T)
+
+F32 = mybir.dt.float32
+BF16 = mybir.dt.bfloat16
+I32 = mybir.dt.int32
+U32 = mybir.dt.uint32
+U16 = mybir.dt.uint16
+U8 = mybir.dt.uint8
+FP8X4 = mybir.dt.float8_e4m3fn_x4
+ALU = mybir.AluOpType
+ACT = mybir.ActivationFunctionType
+
+P = 128
+PACK = 4
+HALF = 512
+VCH = 256
+KEY_CHUNKS = ((0, 512, 256), (512, 256, 256), (768, 256, 128))
+
+
+def tile_attend_brefined_a_kernel(tc, query, fquery, ckeys, fkeys_words, fkeys_scales, share, gout, vals, fac, old, offs, out):
+    nc = tc.nc
+
+    def weave(engine_copy, dst, src):
+        engine_copy(
+            dst.rearrange("p (c i) t -> p c t i", i=4),
+            src.rearrange("p t (c i) -> p c t i", i=4),
+        )
+
+    with ExitStack() as ctx:
+        held = ctx.enter_context(tc.tile_pool(name="held", bufs=1))
+        psum = ctx.enter_context(tc.psum_pool(name="psum", bufs=1))
+
+        def sb(name, shape, dtype, reuse=None):
+            return held.tile(shape, dtype, name=name, tag=reuse or name, align_bytes=64)
+
+        def quantise(codes, scales, woven):
+            nc.vector.quantize_mx(out=codes.bitcast(FP8X4), scales=scales, in_=woven.rearrange("p w t -> p (w t)"))
+
+        offsets = held.tile([P, I // 16], U16, name="offsets")
+        nc.sync.dma_start(offsets[:], offs)
+
+        fk_scales = sb("fk_scales", [P, T], U8)
+        nc.vector.memset(fk_scales[:].bitcast(I32), 0)
+
+        q_raw = sb("q_raw", [P, PACK, Q], F32)
+        nc.sync.dma_start(q_raw[:], query.rearrange("(p j) w -> p j w", j=PACK))
+        ck_view = ckeys.rearrange("(p j) w -> p j w", j=PACK)
+        ck_raw = []
+        for n, (t0, width, by_scalar) in enumerate(KEY_CHUNKS):
+            ck_raw.append(sb(f"ck_raw{n}", [P, PACK, width], F32))
+            nc.sync.dma_start(ck_raw[n][:], ck_view[:, :, t0 : t0 + width])
+            if n == 0:
+                for quad in range(4):
+                    nc.sync.dma_start(
+                        fk_scales[32 * quad : 32 * quad + 8, :].bitcast(I32),
+                        fkeys_scales[:, 4 * quad : 4 * quad + 4, :].bitcast(I32),
+                    )
+        share_col = sb("share_col", [P, 1], F32)
+        nc.sync.dma_start(share_col[:], share)
+        fq_raw = sb("fq_raw", [P, 2, PACK, Q], F32)
+        nc.sync.dma_start(fq_raw[:], fquery.rearrange("(g p j) w -> p g j w", g=2, j=PACK))
+        fk_words = []
+        for g in range(2):
+            fk_words.append(sb(f"fk_words{g}", [P, T], I32))
+            nc.sync.dma_start(fk_words[g][:], fkeys_words[g].rearrange("p n t -> p (n t)").bitcast(I32))
+        fac_col = sb("fac_col", [P, 2, 8], F32)
+        nc.sync.dma_start(fac_col[:, :, 0:PACK], fac.rearrange("o (h p c) -> p (o h) c", h=2, c=PACK))
+        go_raw = sb("go_raw", [P, PACK, Q], F32)
+        nc.sync.dma_start(go_raw[:], gout.rearrange("(p j) w -> p j w", j=PACK))
+        va_view = vals.rearrange("(p j) w -> p j w", j=PACK)
+        n_chunks = T // VCH
+        va_raw = []
+        for c in range(n_chunks):
+            va_raw.append(sb(f"va_raw{c}", [P, PACK, VCH], F32))
+            nc.sync.dma_start(va_raw[c][:], va_view[:, :, c * VCH : (c + 1) * VCH])
+        old_sb = sb("old_sb", [P, T], F32)
+        nc.sync.dma_start(old_sb[:], old)
+
+        ident = sb("ident", [P, P], F32)
+        make_identity(nc, ident[:])
+        zeros = sb("zeros", [P, I], F32)
+        nc.vector.memset(zeros[:], 0.0)
+        ones = sb("ones", [P, I], F32)
+        nc.scalar.activation(ones[:], zeros[:], ACT.Exp)
+        df1 = sb("df1", [P, T], F32)
+        nc.vector.memset(df1[:], 0.0)
+        s1 = sb("s1", [P, T], F32)
+        nc.vector.memset(s1[:], 0.0)
+
+        q_w = sb("q_w", [P, Q, PACK], BF16)
+        weave(nc.vector.tensor_copy, q_w[:], q_raw[:])
+        q_codes = sb("q_codes", [P, Q], U32)
+        q_scales = sb("q_scales", [P, Q], U8)
+        quantise(q_codes[:], q_scales[:], q_w[:])
+
+        a_sb = sb("a_sb", [P, T], F32, reuse="fq_raw")
+        a_ps = [psum.tile([P, HALF], F32, name=f"a_ps{h}", tag=f"bank_a{h}") for h in range(2)]
+        for n, (t0, width, by_scalar) in enumerate(KEY_CHUNKS):
+            ck_w = sb(f"ck_w{n}", [P, width, PACK], BF16, reuse=f"ck_w{n % 2}")
+            weave(nc.scalar.copy, ck_w[:, 0:by_scalar, :], ck_raw[n][:, :, 0:by_scalar])
+            if by_scalar < width:
+                weave(nc.vector.tensor_copy, ck_w[:, by_scalar:width, :], ck_raw[n][:, :, by_scalar:width])
+            ck_codes = sb(f"ck_codes{n}", [P, width], U32)
+            ck_scales = sb(f"ck_scales{n}", [P, width], U8)
+            quantise(ck_codes[:], ck_scales[:], ck_w[:])
+            h, r = divmod(t0, HALF)
+            nc.tensor.matmul_mx(
+                out=a_ps[h][:, r : r + width], lhsT=q_codes[:].bitcast(FP8X4), lhsT_scale=q_scales[:],
+                rhs=ck_codes[:].bitcast(FP8X4), rhs_scale=ck_scales[:], start=True, stop=True,
+            )
+            if r + width == HALF:
+                nc.scalar.copy(a_sb[:, h * HALF : (h + 1) * HALF], a_ps[h][:])
+
+        fq_w = sb("fq_w", [P, 2 * Q, PACK], BF16, reuse="ck_w0")
+        weave(nc.scalar.copy, fq_w[:, 0:Q, :], fq_raw[:, 0, :, :])
+        weave(nc.vector.tensor_copy, fq_w[:, Q : 2 * Q, :], fq_raw[:, 1, :, :])
+        fq_codes = sb("fq_codes", [P, 2 * Q], U32)
+        fq_scales = sb("fq_scales", [P, 2 * Q], U8)
+        quantise(fq_codes[:], fq_scales[:], fq_w[:])
+        fk_scales_g = sb("fk_scales_g", [P, I], U8)
+        nc.vector.tensor_copy(fk_scales_g[:], fk_scales[:].indirect(offsets[:]))
+        neg_share = sb("neg_share", [P, I], F32, reuse="ck_w1")
+        nc.vector.tensor_scalar(neg_share[:], ones[:], share_col[:], -1.0, ALU.mult, ALU.mult)
+        b_ps = psum.tile([P, I], F32, name="b_ps", tag="banks_b")
+        for g in range(2):
+            fk_g = sb(f"fk_g{g}", [P, I], U32, reuse=("ck_w0", "fk_g1")[g])
+            nc.vector.tensor_copy(fk_g[:], fk_words[g][:].bitcast(U32).indirect(offsets[:]))
+            nc.tensor.matmul_mx(
+                out=b_ps[:], lhsT=fq_codes[:, g * Q : (g + 1) * Q].bitcast(FP8X4),
+                lhsT_scale=fq_scales[:, g * Q : (g + 1) * Q],
+                rhs=fk_g[:].bitcast(FP8X4), rhs_scale=fk_scales_g[4 * g : P, :],
+                start=(g == 0), stop=(g == 1),
+            )
+        a_g = sb("a_g", [P, I], F32, reuse="fk_words1")
+        nc.vector.tensor_copy(a_g[:], a_sb[:].indirect(offsets[:]))
+        diff = sb("diff", [P, I], F32)
+        nc.vector.tensor_tensor(diff[:], a_g[:], b_ps[:], ALU.subtract)
+        nc.vector.tensor_tensor(df1[:].indirect(offsets[:]), diff[:], neg_share[:], ALU.mult)
+        fac_ps = psum.tile([P, 2, PACK, P], F32, name="fac_ps", tag="banks_b")
+        for h in range(2):
+            for c in range(PACK):
+                nc.tensor.transpose(fac_ps[:, h, c, :], fac_col[:, h, c : c + 1].to_broadcast([P, P]), ident[:])
+        s_sb = sb("s_sb", [P, T], F32)
+        nc.vector.tensor_tensor(s_sb[:], a_sb[:], df1[:], ALU.add)
+        neg_s = sb("neg_s", [P, T], F32)
+        neg_max = sb("neg_max", [P, 1], F32)
+        nc.vector.tensor_scalar(neg_s[:], s_sb[:], -1.0, None, ALU.mult, ALU.min, accum_out=neg_max[:])
+
+        go_w = sb("go_w", [P, Q, PACK], BF16, reuse="ck_w0")
+        weave(nc.scalar.copy, go_w[:], go_raw[:])
+        go_codes = sb("go_codes", [P, Q], U32, reuse="diff")
+        go_scales = sb("go_scales", [P, Q], U8)
+        quantise(go_codes[:], go_scales[:], go_w[:])
+        c_ps = [psum.tile([P, HALF], F32, name=f"c_ps{h}", tag=f"bank_c{h}") for h in range(2)]
+        va_codes = sb("va_codes", [P, T], U32, reuse="s_sb")
+
+        va_w = sb("va_w", [P, T, PACK], BF16, reuse="go_raw")
+        for c in range(n_chunks):
+            weave(nc.scalar.copy, va_w[:, c * VCH : (c + 1) * VCH, :], va_raw[c][:])
+        for h in range(2):
+            cols = slice(h * HALF, (h + 1) * HALF)
+            va_scales = sb(f"va_scales{h}", [P, HALF], U8)
+            quantise(va_codes[:, cols], va_scales[:], va_w[:, cols, :])
+            nc.tensor.matmul_mx(
+                out=c_ps[h][:], lhsT=go_codes[:].bitcast(FP8X4), lhsT_scale=go_scales[:],
+                rhs=va_codes[:, cols].bitcast(FP8X4), rhs_scale=va_scales[:], start=True, stop=True,
+            )
+
+        p_sb = sb("p_sb", [P, T], F32, reuse=f"va_raw{n_chunks - 1}")
+        z = sb("z", [P, 1], F32)
+        nc.scalar.activation(p_sb[:], neg_s[:], ACT.Exp, bias=neg_max[:], scale=-1.0, accum_out=z[:])
+        rz = sb("rz", [P, 1], F32)
+        nc.vector.reciprocal(rz[:], z[:])
+
+        npf = sb("npf", [P, T], F32)
+
+        def weigh(h, k0, k1):
+            cols = slice(h * HALF + PACK * k0, h * HALF + PACK * k1)
+            nc.vector.scalar_tensor_tensor(
+                npf[:, cols].rearrange("q (k c) -> q k c", c=PACK),
+                p_sb[:, cols].rearrange("q (k c) -> q k c", c=PACK),
+                -1024.0,
+                fac_ps[:, h, :, k0:k1].rearrange("q c k -> q k c"),
+                ALU.mult, ALU.mult,
+            )
+
+        for h in range(2):
+            weigh(h, 0, P)
+        nu = sb("nu", [P, T], F32)
+        s_parts = [sb(f"sum{h}", [P, 1], F32) for h in range(2)]
+        for h in range(2):
+            cols = slice(h * HALF, (h + 1) * HALF)
+            nc.vector.scalar_tensor_tensor(
+                nu[:, cols], c_ps[h][:], rz[:], npf[:, cols], ALU.mult, ALU.mult, accum_out=s_parts[h][:]
+            )
+        dz = sb("dz", [P, 1], F32)
+        nc.vector.tensor_scalar(dz[:], s_parts[0][:], s_parts[1][:], rz[:], ALU.add, ALU.mult)
+        turned_ps = [psum.tile([P, PACK, P], F32, name=f"turned_ps{h}", tag=f"bank_c{h}") for h in range(2)]
+        base_ps = [psum.tile([P, PACK, P], F32, name=f"base_ps{h}", tag=f"bank_a{h}") for h in range(2)]
+
+        def turn(dst, src, h, start, stop):
+            for c in range(PACK):
+                c0 = h * HALF + c * P
+                nc.tensor.matmul(
+                    dst[:, c, :], src[:, c0 : c0 + P], ident[:], is_transpose=True,
+                    start=(start and c == 0), stop=(stop and c == PACK - 1),
+                )
+
+        for h in range(2):
+            turn(turned_ps[h], old_sb, h, True, False)
+        ds = sb("ds", [P, T], F32)
+        turned = sb("turned", [P, T], F32)
+        for h in range(2):
+            cols = slice(h * HALF, (h + 1) * HALF)
+            nc.vector.scalar_tensor_tensor(ds[:, cols], p_sb[:, cols], dz[:], nu[:, cols], ALU.mult, ALU.subtract)
+            turn(turned_ps[h], ds, h, False, True)
+            nc.scalar.copy(turned[:, cols], turned_ps[h][:].rearrange("p c q -> p (c q)"))
+        for h in range(2):
+            turn(base_ps[h], turned, h, True, True)
+
+        ds_g = sb("ds_g", [P, I], F32)
+        nc.vector.tensor_copy(ds_g[:], ds[:].indirect(offsets[:]))
+        nc.vector.tensor_tensor(s1[:].indirect(offsets[:]), ds_g[:], neg_share[:], ALU.mult)
+        for n, (t0, width) in enumerate(((0, 512), (512, 256), (768, 256))):
+            h, r = divmod(t0, HALF)
+            cols = slice(t0, t0 + width)
+            y = sb(f"y{n}", [P, width], F32)
+            nc.vector.tensor_tensor(
+                y[:], base_ps[h][:].rearrange("p c q -> p (c q)")[:, r : r + width], s1[:, cols], ALU.add
+            )
+            nc.sync.dma_start(out[:, cols], y[:])

@@ -43,7 +43,6 @@ def tile_attend_brefined_a_kernel(tc, query, fquery, ckeys, fkeys_words, fkeys_s
             nc.vector.quantize_mx(out=codes.bitcast(FP8X4), scales=scales, in_=woven.rearrange("p w t -> p (w t)"))
 
         offsets = held.tile([P, I // 16], U16, name="offsets")
-        nc.sync.dma_start(offsets[:], offs)
 
         fk_scales = sb("fk_scales", [P, T], U8)
         nc.vector.memset(fk_scales[:].bitcast(I32), 0)
@@ -56,6 +55,7 @@ def tile_attend_brefined_a_kernel(tc, query, fquery, ckeys, fkeys_words, fkeys_s
             ck_raw.append(sb(f"ck_raw{n}", [P, PACK, width], F32))
             nc.sync.dma_start(ck_raw[n][:], ck_view[:, :, t0 : t0 + width])
             if n == 0:
+                nc.sync.dma_start(offsets[:], offs)
                 for quad in range(4):
                     nc.sync.dma_start(
                         fk_scales[32 * quad : 32 * quad + 8, :].bitcast(I32),
@@ -148,17 +148,16 @@ def tile_attend_brefined_a_kernel(tc, query, fquery, ckeys, fkeys_words, fkeys_s
                 nc.tensor.transpose(fac_ps[:, h, c, :], fac_col[:, h, c : c + 1].to_broadcast([P, P]), ident[:])
         s_sb = sb("s_sb", [P, T], F32)
         nc.vector.tensor_tensor(s_sb[:], a_sb[:], df1[:], ALU.add)
-        neg_s = sb("neg_s", [P, T], F32)
         neg_max = sb("neg_max", [P, 1], F32)
-        nc.vector.tensor_scalar(neg_s[:], s_sb[:], -1.0, None, ALU.mult, ALU.min, accum_out=neg_max[:])
+        nc.vector.tensor_reduce(neg_max[:], s_sb[:], mybir.AxisListType.X, ALU.max, negate=True)
 
         go_w = sb("go_w", [P, Q, PACK], BF16, reuse="ck_w0")
         weave(nc.scalar.copy, go_w[:], go_raw[:])
-        go_codes = sb("go_codes", [P, Q], U32, reuse="diff")
+        go_codes = sb("go_codes", [P, Q], U32)
         go_scales = sb("go_scales", [P, Q], U8)
         quantise(go_codes[:], go_scales[:], go_w[:])
         c_ps = [psum.tile([P, HALF], F32, name=f"c_ps{h}", tag=f"bank_c{h}") for h in range(2)]
-        va_codes = sb("va_codes", [P, T], U32, reuse="s_sb")
+        va_codes = sb("va_codes", [P, T], U32, reuse="fq_raw")
 
         va_w = sb("va_w", [P, T, PACK], BF16, reuse="go_raw")
         for c in range(n_chunks):
@@ -173,10 +172,13 @@ def tile_attend_brefined_a_kernel(tc, query, fquery, ckeys, fkeys_words, fkeys_s
             )
 
         p_sb = sb("p_sb", [P, T], F32, reuse=f"va_raw{n_chunks - 1}")
+        z_parts = [sb(f"z{h}", [P, 1], F32) for h in range(2)]
+        for h in range(2):
+            cols = slice(h * HALF, (h + 1) * HALF)
+            nc.scalar.activation(p_sb[:, cols], s_sb[:, cols], ACT.Exp, bias=neg_max[:], accum_out=z_parts[h][:])
         z = sb("z", [P, 1], F32)
-        nc.scalar.activation(p_sb[:], neg_s[:], ACT.Exp, bias=neg_max[:], scale=-1.0, accum_out=z[:])
+        nc.scalar.activation(z[:], z_parts[0][:], ACT.Identity, bias=z_parts[1][:])
         rz = sb("rz", [P, 1], F32)
-        nc.vector.reciprocal(rz[:], z[:])
 
         npf = sb("npf", [P, T], F32)
 
@@ -190,8 +192,9 @@ def tile_attend_brefined_a_kernel(tc, query, fquery, ckeys, fkeys_words, fkeys_s
                 ALU.mult, ALU.mult,
             )
 
-        for h in range(2):
-            weigh(h, 0, P)
+        weigh(0, 0, P)
+        nc.vector.reciprocal(rz[:], z[:])
+        weigh(1, 0, P)
         nu = sb("nu", [P, T], F32)
         s_parts = [sb(f"sum{h}", [P, 1], F32) for h in range(2)]
         for h in range(2):
@@ -201,37 +204,36 @@ def tile_attend_brefined_a_kernel(tc, query, fquery, ckeys, fkeys_words, fkeys_s
             )
         dz = sb("dz", [P, 1], F32)
         nc.vector.tensor_scalar(dz[:], s_parts[0][:], s_parts[1][:], rz[:], ALU.add, ALU.mult)
-        turned_ps = [psum.tile([P, PACK, P], F32, name=f"turned_ps{h}", tag=f"bank_c{h}") for h in range(2)]
-        base_ps = [psum.tile([P, PACK, P], F32, name=f"base_ps{h}", tag=f"bank_a{h}") for h in range(2)]
+        turned_ps = psum.tile([P, PACK, P], F32, name="turned_ps", tag="bank_c0")
+        base_ps = psum.tile([P, PACK, P], F32, name="base_ps", tag="bank_a0")
 
-        def turn(dst, src, h, start, stop):
+        def turn(dst, src, start, stop):
             for c in range(PACK):
-                c0 = h * HALF + c * P
                 nc.tensor.matmul(
-                    dst[:, c, :], src[:, c0 : c0 + P], ident[:], is_transpose=True,
+                    dst[:, c, :], src[:, c * P : (c + 1) * P], ident[:], is_transpose=True,
                     start=(start and c == 0), stop=(stop and c == PACK - 1),
                 )
 
-        for h in range(2):
-            turn(turned_ps[h], old_sb, h, True, False)
+        turn(turned_ps, old_sb, True, False)
         ds = sb("ds", [P, T], F32)
-        turned = sb("turned", [P, T], F32)
-        for h in range(2):
-            cols = slice(h * HALF, (h + 1) * HALF)
+        pieces = (slice(0, 512), slice(512, 768), slice(768, 1024))
+        for cols in pieces:
             nc.vector.scalar_tensor_tensor(ds[:, cols], p_sb[:, cols], dz[:], nu[:, cols], ALU.mult, ALU.subtract)
-            turn(turned_ps[h], ds, h, False, True)
-            nc.scalar.copy(turned[:, cols], turned_ps[h][:].rearrange("p c q -> p (c q)"))
-        for h in range(2):
-            turn(base_ps[h], turned, h, True, True)
+        turn(turned_ps, ds, False, True)
+        turned = sb("turned", [P, HALF], F32)
+        nc.scalar.copy(turned[:], turned_ps[:].rearrange("p c q -> p (c q)"))
+        turn(base_ps, turned, True, True)
 
+        base = sb("base", [P, T], F32)
         ds_g = sb("ds_g", [P, I], F32)
+        nc.vector.tensor_tensor(base[:, pieces[1]], ds[:, pieces[1]], old_sb[:, pieces[1]], ALU.add)
         nc.vector.tensor_copy(ds_g[:], ds[:].indirect(offsets[:]))
+        nc.vector.tensor_tensor(base[:, pieces[2]], ds[:, pieces[2]], old_sb[:, pieces[2]], ALU.add)
         nc.vector.tensor_tensor(s1[:].indirect(offsets[:]), ds_g[:], neg_share[:], ALU.mult)
-        for n, (t0, width) in enumerate(((0, 512), (512, 256), (768, 256))):
-            h, r = divmod(t0, HALF)
-            cols = slice(t0, t0 + width)
-            y = sb(f"y{n}", [P, width], F32)
-            nc.vector.tensor_tensor(
-                y[:], base_ps[h][:].rearrange("p c q -> p (c q)")[:, r : r + width], s1[:, cols], ALU.add
-            )
+        base0 = base_ps[:].rearrange("p c q -> p (c q)")
+        for n, (cols, src) in enumerate(
+            ((slice(HALF, T), base[:, HALF:T]), (slice(0, 256), base0[:, 0:256]), (slice(256, 512), base0[:, 256:512]))
+        ):
+            y = sb(f"y{n}", [P, cols.stop - cols.start], F32)
+            nc.vector.tensor_tensor(y[:], src, s1[:, cols], ALU.add)
             nc.sync.dma_start(out[:, cols], y[:])

from contextlib import ExitStack

import concourse.mybir as mybir
from concourse.masks import make_identity

D, K, E, T, I, Q = 512, 1024, 512, 1024, 256, 128
FLOPS = 2 * Q * (D * T + K * I + E * T)

F32 = mybir.dt.float32
BF16 = mybir.dt.bfloat16
I32 = mybir.dt.int32
U32 = mybir.dt.uint32
U16 = mybir.dt.uint16
U8 = mybir.dt.uint8
FP8X4 = mybir.dt.float8_e4m3fn_x4
ALU = mybir.AluOpType
ACT = mybir.ActivationFunctionType

P = 128
PACK = 4
HALF = 512
VCH = 256
KEY_CHUNKS = ((0, 512, 256), (512, 256, 256), (768, 256, 128))


def tile_attend_brefined_a_kernel(tc, query, fquery, ckeys, fkeys_words, fkeys_scales, share, gout, vals, fac, old, offs, out):
    nc = tc.nc

    def weave(engine_copy, dst, src):
        engine_copy(
            dst.rearrange("p (c i) t -> p c t i", i=4),
            src.rearrange("p t (c i) -> p c t i", i=4),
        )

    with ExitStack() as ctx:
        held = ctx.enter_context(tc.tile_pool(name="held", bufs=1))
        psum = ctx.enter_context(tc.psum_pool(name="psum", bufs=1))

        def sb(name, shape, dtype, reuse=None):
            return held.tile(shape, dtype, name=name, tag=reuse or name, align_bytes=64)

        def quantise(codes, scales, woven):
            nc.vector.quantize_mx(out=codes.bitcast(FP8X4), scales=scales, in_=woven.rearrange("p w t -> p (w t)"))

        offsets = held.tile([P, I // 16], U16, name="offsets")

        fk_scales = sb("fk_scales", [P, T], U8)
        nc.vector.memset(fk_scales[:].bitcast(I32), 0)

        q_raw = sb("q_raw", [P, PACK, Q], F32)
        nc.sync.dma_start(q_raw[:], query.rearrange("(p j) w -> p j w", j=PACK))
        ck_view = ckeys.rearrange("(p j) w -> p j w", j=PACK)
        ck_raw = []
        for n, (t0, width, by_scalar) in enumerate(KEY_CHUNKS):
            ck_raw.append(sb(f"ck_raw{n}", [P, PACK, width], F32))
            nc.sync.dma_start(ck_raw[n][:], ck_view[:, :, t0 : t0 + width])
            if n == 0:
                nc.sync.dma_start(offsets[:], offs)
                for quad in range(4):
                    nc.sync.dma_start(
                        fk_scales[32 * quad : 32 * quad + 8, :].bitcast(I32),
                        fkeys_scales[:, 4 * quad : 4 * quad + 4, :].bitcast(I32),
                    )
        share_col = sb("share_col", [P, 1], F32)
        nc.sync.dma_start(share_col[:], share)
        fq_raw = sb("fq_raw", [P, 2, PACK, Q], F32)
        nc.sync.dma_start(fq_raw[:], fquery.rearrange("(g p j) w -> p g j w", g=2, j=PACK))
        fk_words = []
        for g in range(2):
            fk_words.append(sb(f"fk_words{g}", [P, T], I32))
            nc.sync.dma_start(fk_words[g][:], fkeys_words[g].rearrange("p n t -> p (n t)").bitcast(I32))
        fac_col = sb("fac_col", [P, 2, 8], F32)
        nc.sync.dma_start(fac_col[:, :, 0:PACK], fac.rearrange("o (h p c) -> p (o h) c", h=2, c=PACK))
        go_raw = sb("go_raw", [P, PACK, Q], F32)
        nc.sync.dma_start(go_raw[:], gout.rearrange("(p j) w -> p j w", j=PACK))
        va_view = vals.rearrange("(p j) w -> p j w", j=PACK)
        n_chunks = T // VCH
        va_raw = []
        for c in range(n_chunks):
            va_raw.append(sb(f"va_raw{c}", [P, PACK, VCH], F32))
            nc.sync.dma_start(va_raw[c][:], va_view[:, :, c * VCH : (c + 1) * VCH])
        old_sb = sb("old_sb", [P, T], F32)
        nc.sync.dma_start(old_sb[:], old)

        ident = sb("ident", [P, P], F32)
        make_identity(nc, ident[:])
        zeros = sb("zeros", [P, I], F32)
        nc.vector.memset(zeros[:], 0.0)
        ones = sb("ones", [P, I], F32)
        nc.scalar.activation(ones[:], zeros[:], ACT.Exp)
        df1 = sb("df1", [P, T], F32)
        nc.vector.memset(df1[:], 0.0)
        s1 = sb("s1", [P, T], F32)
        nc.vector.memset(s1[:], 0.0)

        q_w = sb("q_w", [P, Q, PACK], BF16)
        weave(nc.vector.tensor_copy, q_w[:], q_raw[:])
        q_codes = sb("q_codes", [P, Q], U32)
        q_scales = sb("q_scales", [P, Q], U8)
        quantise(q_codes[:], q_scales[:], q_w[:])

        a_sb = sb("a_sb", [P, T], F32, reuse="fq_raw")
        a_ps = [psum.tile([P, HALF], F32, name=f"a_ps{h}", tag=f"bank_a{h}") for h in range(2)]
        for n, (t0, width, by_scalar) in enumerate(KEY_CHUNKS):
            ck_w = sb(f"ck_w{n}", [P, width, PACK], BF16, reuse=f"ck_w{n % 2}")
            weave(nc.scalar.copy, ck_w[:, 0:by_scalar, :], ck_raw[n][:, :, 0:by_scalar])
            if by_scalar < width:
                weave(nc.vector.tensor_copy, ck_w[:, by_scalar:width, :], ck_raw[n][:, :, by_scalar:width])
            ck_codes = sb(f"ck_codes{n}", [P, width], U32)
            ck_scales = sb(f"ck_scales{n}", [P, width], U8)
            quantise(ck_codes[:], ck_scales[:], ck_w[:])
            h, r = divmod(t0, HALF)
            nc.tensor.matmul_mx(
                out=a_ps[h][:, r : r + width], lhsT=q_codes[:].bitcast(FP8X4), lhsT_scale=q_scales[:],
                rhs=ck_codes[:].bitcast(FP8X4), rhs_scale=ck_scales[:], start=True, stop=True,
            )
            if r + width == HALF:
                nc.scalar.copy(a_sb[:, h * HALF : (h + 1) * HALF], a_ps[h][:])

        fq_w = sb("fq_w", [P, 2 * Q, PACK], BF16, reuse="ck_w0")
        weave(nc.scalar.copy, fq_w[:, 0:Q, :], fq_raw[:, 0, :, :])
        weave(nc.vector.tensor_copy, fq_w[:, Q : 2 * Q, :], fq_raw[:, 1, :, :])
        fq_codes = sb("fq_codes", [P, 2 * Q], U32)
        fq_scales = sb("fq_scales", [P, 2 * Q], U8)
        quantise(fq_codes[:], fq_scales[:], fq_w[:])
        fk_scales_g = sb("fk_scales_g", [P, I], U8)
        nc.vector.tensor_copy(fk_scales_g[:], fk_scales[:].indirect(offsets[:]))
        neg_share = sb("neg_share", [P, I], F32, reuse="ck_w1")
        nc.vector.tensor_scalar(neg_share[:], ones[:], share_col[:], -1.0, ALU.mult, ALU.mult)
        b_ps = psum.tile([P, I], F32, name="b_ps", tag="banks_b")
        for g in range(2):
            fk_g = sb(f"fk_g{g}", [P, I], U32, reuse=("ck_w0", "fk_g1")[g])
            nc.vector.tensor_copy(fk_g[:], fk_words[g][:].bitcast(U32).indirect(offsets[:]))
            nc.tensor.matmul_mx(
                out=b_ps[:], lhsT=fq_codes[:, g * Q : (g + 1) * Q].bitcast(FP8X4),
                lhsT_scale=fq_scales[:, g * Q : (g + 1) * Q],
                rhs=fk_g[:].bitcast(FP8X4), rhs_scale=fk_scales_g[4 * g : P, :],
                start=(g == 0), stop=(g == 1),
            )
        a_g = sb("a_g", [P, I], F32, reuse="fk_words1")
        nc.vector.tensor_copy(a_g[:], a_sb[:].indirect(offsets[:]))
        diff = sb("diff", [P, I], F32)
        nc.vector.tensor_tensor(diff[:], a_g[:], b_ps[:], ALU.subtract)
        nc.vector.tensor_tensor(df1[:].indirect(offsets[:]), diff[:], neg_share[:], ALU.mult)
        fac_ps = psum.tile([P, 2, PACK, P], F32, name="fac_ps", tag="banks_b")
        for h in range(2):
            for c in range(PACK):
                nc.tensor.transpose(fac_ps[:, h, c, :], fac_col[:, h, c : c + 1].to_broadcast([P, P]), ident[:])
        s_sb = sb("s_sb", [P, T], F32)
        nc.vector.tensor_tensor(s_sb[:], a_sb[:], df1[:], ALU.add)
        neg_max = sb("neg_max", [P, 1], F32)
        nc.vector.tensor_reduce(neg_max[:], s_sb[:], mybir.AxisListType.X, ALU.max, negate=True)

        go_w = sb("go_w", [P, Q, PACK], BF16, reuse="ck_w0")
        weave(nc.scalar.copy, go_w[:], go_raw[:])
        go_codes = sb("go_codes", [P, Q], U32)
        go_scales = sb("go_scales", [P, Q], U8)
        quantise(go_codes[:], go_scales[:], go_w[:])
        c_ps = [psum.tile([P, HALF], F32, name=f"c_ps{h}", tag=f"bank_c{h}") for h in range(2)]
        va_codes = sb("va_codes", [P, T], U32, reuse="fq_raw")

        va_w = sb("va_w", [P, T, PACK], BF16, reuse="go_raw")
        for c in range(n_chunks):
            weave(nc.scalar.copy, va_w[:, c * VCH : (c + 1) * VCH, :], va_raw[c][:])
        for h in range(2):
            cols = slice(h * HALF, (h + 1) * HALF)
            va_scales = sb(f"va_scales{h}", [P, HALF], U8)
            quantise(va_codes[:, cols], va_scales[:], va_w[:, cols, :])
            nc.tensor.matmul_mx(
                out=c_ps[h][:], lhsT=go_codes[:].bitcast(FP8X4), lhsT_scale=go_scales[:],
                rhs=va_codes[:, cols].bitcast(FP8X4), rhs_scale=va_scales[:], start=True, stop=True,
            )

        p_sb = sb("p_sb", [P, T], F32, reuse=f"va_raw{n_chunks - 1}")
        z_parts = [sb(f"z{h}", [P, 1], F32) for h in range(2)]
        for h in range(2):
            cols = slice(h * HALF, (h + 1) * HALF)
            nc.scalar.activation(p_sb[:, cols], s_sb[:, cols], ACT.Exp, bias=neg_max[:], accum_out=z_parts[h][:])
        z = sb("z", [P, 1], F32)
        nc.scalar.activation(z[:], z_parts[0][:], ACT.Identity, bias=z_parts[1][:])
        rz = sb("rz", [P, 1], F32)

        npf = sb("npf", [P, T], F32)

        def weigh(h, k0, k1):
            cols = slice(h * HALF + PACK * k0, h * HALF + PACK * k1)
            nc.vector.scalar_tensor_tensor(
                npf[:, cols].rearrange("q (k c) -> q k c", c=PACK),
                p_sb[:, cols].rearrange("q (k c) -> q k c", c=PACK),
                -1024.0,
                fac_ps[:, h, :, k0:k1].rearrange("q c k -> q k c"),
                ALU.mult, ALU.mult,
            )

        weigh(0, 0, P)
        nc.vector.reciprocal(rz[:], z[:])
        weigh(1, 0, P)
        nu = sb("nu", [P, T], F32)
        s_parts = [sb(f"sum{h}", [P, 1], F32) for h in range(2)]
        for h in range(2):
            cols = slice(h * HALF, (h + 1) * HALF)
            nc.vector.scalar_tensor_tensor(
                nu[:, cols], c_ps[h][:], rz[:], npf[:, cols], ALU.mult, ALU.mult, accum_out=s_parts[h][:]
            )
        dz = sb("dz", [P, 1], F32)
        nc.vector.tensor_scalar(dz[:], s_parts[0][:], s_parts[1][:], rz[:], ALU.add, ALU.mult)
        turned_ps = psum.tile([P, PACK, P], F32, name="turned_ps", tag="bank_c0")
        base_ps = psum.tile([P, PACK, P], F32, name="base_ps", tag="bank_a0")

        def turn(dst, src, start, stop):
            for c in range(PACK):
                nc.tensor.matmul(
                    dst[:, c, :], src[:, c * P : (c + 1) * P], ident[:], is_transpose=True,
                    start=(start and c == 0), stop=(stop and c == PACK - 1),
                )

        turn(turned_ps, old_sb, True, False)
        ds = sb("ds", [P, T], F32)
        pieces = (slice(0, 512), slice(512, 768), slice(768, 1024))
        for cols in pieces:
            nc.vector.scalar_tensor_tensor(ds[:, cols], p_sb[:, cols], dz[:], nu[:, cols], ALU.mult, ALU.subtract)
        turn(turned_ps, ds, False, True)
        turned = sb("turned", [P, HALF], F32)
        nc.scalar.copy(turned[:], turned_ps[:].rearrange("p c q -> p (c q)"))
        turn(base_ps, turned, True, True)

        base = sb("base", [P, T], F32)
        ds_g = sb("ds_g", [P, I], F32)
        nc.vector.tensor_tensor(base[:, pieces[1]], ds[:, pieces[1]], old_sb[:, pieces[1]], ALU.add)
        nc.vector.tensor_copy(ds_g[:], ds[:].indirect(offsets[:]))
        nc.vector.tensor_tensor(base[:, pieces[2]], ds[:, pieces[2]], old_sb[:, pieces[2]], ALU.add)
        nc.vector.tensor_tensor(s1[:].indirect(offsets[:]), ds_g[:], neg_share[:], ALU.mult)
        base0 = base_ps[:].rearrange("p c q -> p (c q)")
        for n, (cols, src) in enumerate(
            ((slice(HALF, T), base[:, HALF:T]), (slice(0, 256), base0[:, 0:256]), (slice(256, 512), base0[:, 256:512]))
        ):
            y = sb(f"y{n}", [P, cols.stop - cols.start], F32)
            nc.vector.tensor_tensor(y[:], src, s1[:, cols], ALU.add)
            nc.sync.dma_start(out[:, cols], y[:])
